import numpy as np
import ml_dtypes


def mxq(x, axis, fmt="e4m3"):
    dtype, down = {"e4m3": (ml_dtypes.float8_e4m3fn, 7), "e5m2": (ml_dtypes.float8_e5m2, 14)}[fmt]
    v = np.moveaxis(np.asarray(x, np.float32).astype(ml_dtypes.bfloat16).astype(np.float64), axis, -1)
    blocks = v.reshape(v.shape[:-1] + (-1, 32))
    amax = np.abs(blocks).max(-1, keepdims=True)
    byte = np.maximum(np.where(amax > 0, np.frexp(amax)[1] - 1 + 127, 0) - down, 1)
    scale = np.exp2(byte - 127.0)
    codes = (blocks / scale).astype(np.float32).astype(dtype).astype(np.float64)
    return np.moveaxis((codes * scale).reshape(v.shape), -1, axis)


WIDE = False


def mx_kscale(k):
    if not WIDE:
        return np.ones(k)
    levels = np.array([10, -10, 5, -5, 0])
    if k % 512:
        return np.exp2(np.random.permutation(np.resize(levels, k // 32))).repeat(32)
    a = np.empty((k // 512, 16))
    for p in range(k // 512):
        a[p, :8] = np.random.permutation(np.resize(levels, 8))
        for g in range(8):
            far = levels[np.abs(levels - a[p, g]) >= 10]
            a[p, g + 8] = far[np.random.randint(len(far))]
    return np.exp2(a.ravel()).repeat(32)


def f64(x):
    return np.asarray(x).astype(np.float64)


def striped8(idx):
    return np.asarray(idx).reshape(8, -1, 16).transpose(0, 2, 1).reshape(128, -1).astype(np.uint16)


def unstriped8(offs):
    return offs.reshape(8, 16, -1).transpose(0, 2, 1).reshape(8, -1).astype(np.int64)


def pick8(x, idx, run):
    r = np.arange(len(x))
    return x[r[:, None], idx[r % (8 * run) // run]]


E2M1 = np.array([0.0, 0.5, 1.0, 1.5, 2.0, 3.0, 4.0, 6.0, -0.0, -0.5, -1.0, -1.5, -2.0, -3.0, -4.0, -6.0])


def pack_weight(w, fmt):
    k, n = w.shape
    w = f64(np.asarray(w, np.float32).astype(ml_dtypes.bfloat16)).reshape(k // 32, 32, n)
    amax = np.abs(w).max(1)
    if fmt == "e4m3":
        byte = np.frexp(amax)[1] - 1 + 127 - 7
    else:
        mant, ex = np.frexp(amax / 6.0)
        byte = np.where(mant > 0.5, ex, ex - 1) + 127
    byte = np.clip(np.where(amax > 0, byte, 1), 1, 254)
    scaled = (w * np.exp2(127.0 - byte)[:, None, :]).reshape(k, n).astype(np.float32)
    by_word = np.ascontiguousarray(scaled.reshape(k // 512, 128, 4, n).transpose(0, 1, 3, 2))
    if fmt == "e4m3":
        words = by_word.astype(ml_dtypes.float8_e4m3fn).view(np.uint8)
    else:
        c = by_word.astype(ml_dtypes.float4_e2m1fn).view(np.uint8) & 0xF
        words = (c[..., 0::2] | (c[..., 1::2] << 4)).reshape(k // 512, 128, 2 * n)
    return np.ascontiguousarray(words), np.ascontiguousarray(byte.astype(np.uint8).reshape(k // 512, 16, n))


def unpack_weight(words, scales, fmt):
    g, _, n = scales.shape
    words = np.ascontiguousarray(words).reshape(g, 128, n, -1)
    if fmt == "e4m3":
        vals = words.view(ml_dtypes.float8_e4m3fn).astype(np.float64)
    else:
        nib = np.empty((g, 128, n, 4), np.uint8)
        nib[..., 0::2] = words & 0xF
        nib[..., 1::2] = words >> 4
        vals = E2M1[nib]
    vals = vals * np.repeat(np.exp2(scales.astype(np.float64) - 127.0), 8, axis=1)[..., None]
    return vals.transpose(0, 1, 3, 2).reshape(g * 512, n)


D, K, T, I, Q = 512, 512, 1024, 512, 128


def setup_inputs():
    n = np.random.standard_normal
    idx = np.stack([np.random.permutation(T)[:I] for _ in range(8)])
    idx2 = np.stack([np.random.permutation(T)[:I] for _ in range(8)])
    idx3 = np.stack([np.random.permutation(T)[:I] for _ in range(8)])
    idx4 = np.stack([np.random.permutation(T)[:I] for _ in range(8)])
    idx5 = np.stack([np.random.permutation(T)[:I] for _ in range(8)])
    fd = mx_kscale(D)
    fk = mx_kscale(K)
    wqp = pack_weight(n((D, K)) * 1.0 / np.sqrt(D) * fd[:, None] * fk, "e4m3")
    cachep = pack_weight(n((K, T)) * 1.0 / np.sqrt(K) / fk[:, None], "e4m3")
    tagsp = pack_weight(n((D, T)) * 0.5 / np.sqrt(D) * fd[:, None], "e2m1")
    return {
        "states": (n((D, Q)) * 0.95 / fd[:, None]).astype(np.float32),
        "wq_words": wqp[0],
        "wq_scales": wqp[1],
        "cache_words": cachep[0],
        "cache_scales": cachep[1],
        "tags_words": tagsp[0],
        "tags_scales": tagsp[1],
        "offs": striped8(idx),
        "offs2": striped8(idx2),
        "offs3": striped8(idx3),
        "offs4": striped8(idx4),
        "offs5": striped8(idx5),
    }


def reference(states, wq_words, wq_scales, cache_words, cache_scales, tags_words, tags_scales, offs, offs2, offs3, offs4, offs5):
    idx = unstriped8(offs)
    idx2 = unstriped8(offs2)
    idx3 = unstriped8(offs3)
    idx4 = unstriped8(offs4)
    idx5 = unstriped8(offs5)
    wqu = unpack_weight(wq_words, wq_scales, "e4m3")
    cacheu = unpack_weight(cache_words, cache_scales, "e4m3")
    tagsu = unpack_weight(tags_words, tags_scales, "e2m1")
    statesq = mxq(f64(states), 0, "e4m3")
    qv = wqu.T @ statesq
    qvq = mxq(qv, 0, "e4m3")
    a = qvq.T @ cacheu + statesq.T @ tagsu
    a1 = np.pad(a, ((0, 0), (1, 0)))[:, :T]
    w = np.maximum(pick8(a1, idx, 16), pick8(a, idx2, 16))
    f1 = np.zeros((Q, T))
    f1[np.arange(Q)[:, None], idx3[np.arange(Q) % 128 // 16]] = w
    f2 = np.zeros((Q, T))
    f2[np.arange(Q)[:, None], idx4[np.arange(Q) % 128 // 16]] = pick8(a1, idx, 16)
    c1 = a - f1
    c2 = np.maximum(c1, f2)
    y = pick8(c2, idx5, 16) + pick8(a1, idx2, 16)
    return y

@@ -1,0 +1,186 @@
+from contextlib import ExitStack
+
+import concourse.mybir as mybir
+
+D, K, T, I, Q = 512, 512, 1024, 512, 128
+FLOPS = 2 * (D * K * Q + K * Q * T + D * Q * T)
+
+F32 = mybir.dt.float32
+BF16 = mybir.dt.bfloat16
+I32 = mybir.dt.int32
+U32 = mybir.dt.uint32
+U16 = mybir.dt.uint16
+U8 = mybir.dt.uint8
+FP8X4 = mybir.dt.float8_e4m3fn_x4
+FP4X4 = mybir.dt.float4_e2m1fn_x4
+COPY = mybir.ActivationFunctionType.Copy
+ALU = mybir.AluOpType
+
+P = 128
+PACK = 4
+BANKS = 4
+NB = T // BANKS
+HALF = I // 2
+LANES = 16
+
+
+def entries(list_tile, lo, hi):
+    return list_tile[:, lo // LANES : hi // LANES]
+
+
+def tile_attend_nexttoken_parts_kernel(
+    tc, states, wq_words, wq_scales, cache_words, cache_scales, tags_words, tags_scales,
+    offs, offs2, offs3, offs4, offs5, out,
+):
+    nc = tc.nc
+    with ExitStack() as ctx:
+        lists = ctx.enter_context(tc.tile_pool(name="lists", bufs=1))
+        sb = ctx.enter_context(tc.tile_pool(name="sb", bufs=1))
+        psum = ctx.enter_context(tc.psum_pool(name="psum", bufs=1))
+
+        def scale_tile(name, width):
+            plane = sb.tile([P, 2 * width], U8, name=name, align_bytes=64)
+            nc.vector.memset(plane[:].bitcast(I32), 0)
+            return plane
+
+        def load_scales(queue, plane, scales):
+            rows = scales[0].bitcast(I32).rearrange("(h g r) n -> g r h n", h=2, g=2)
+            for g in range(2):
+                queue.dma_start(
+                    plane[32 * g : 32 * g + 4, :].bitcast(I32).rearrange("r (h n) -> r h n", h=2), rows[g]
+                )
+
+        def spread_scales(plane, width):
+            words = plane[:].bitcast(I32)
+            n = width // 4
+            nc.vector.tensor_copy(words[64:128, 0:n], words[0:64, n : 2 * n])
+
+        wq_sc = scale_tile("wq_sc", K)
+        tags_sc = scale_tile("tags_sc", T)
+        cache_sc = scale_tile("cache_sc", T)
+        zero = sb.tile([P, 1], F32, name="zero")
+        nc.vector.memset(zero[:], 0.0)
+        f1 = sb.tile([P, T], F32, name="f1")
+        f2 = sb.tile([P, T], F32, name="f2")
+        nc.vector.memset(f2[:], 0.0)
+        nc.vector.memset(f1[:], 0.0)
+
+        states_raw = sb.tile([P, PACK, Q], F32, name="states_raw")
+        nc.sync.dma_start(states_raw[:], states.rearrange("(p t) q -> p t q", t=PACK))
+        load_scales(nc.scalar, wq_sc, wq_scales)
+        wq_raw = sb.tile([P, K], U32, name="wq_raw")
+        nc.sync.dma_start(wq_raw[:].bitcast(I32), wq_words[0].rearrange("p n t -> p (n t)").bitcast(I32))
+        load_scales(nc.scalar, tags_sc, tags_scales)
+        tags_w = sb.tile([P, 2 * T], U8, name="tags_w", align_bytes=64)
+        nc.sync.dma_start(tags_w[:].bitcast(I32), tags_words[0].bitcast(I32))
+        load_scales(nc.sync, cache_sc, cache_scales)
+        cache_w = sb.tile([P, T], U32, name="cache_w", align_bytes=64)
+        nc.sync.dma_start(cache_w[:].bitcast(I32), cache_words[0].rearrange("p n t -> p (n t)").bitcast(I32))
+        held = []
+        for name, src in (("idx", offs), ("idx4", offs4), ("idx2", offs2), ("idx3", offs3), ("idx5", offs5)):
+            list_tile = lists.tile([P, I // LANES], U16, name=name)
+            nc.sync.dma_start(list_tile[:], src)
+            held.append(list_tile)
+        idx, idx4, idx2, idx3, idx5 = held
+
+        a = sb.tile([P, T], F32, name="a")
+        a1 = sb.tile([P, T], F32, name="a1")
+        nc.scalar.activation(a1[:, 0:1], zero[:], COPY)
+
+        spread_scales(wq_sc, K)
+        states_bf = sb.tile([P, Q, PACK], BF16, name="states_bf", align_bytes=64)
+        nc.vector.tensor_copy(states_bf[:], states_raw[:].rearrange("p t q -> p q t"))
+        wq_sc_dealt = sb.tile([P, K], U8, name="wq_sc_dealt", align_bytes=64)
+        nc.vector.tensor_copy(
+            wq_sc_dealt[:].rearrange("p (t m) -> p m t", t=PACK),
+            wq_sc[:, 0:K].rearrange("p (m t) -> p m t", t=PACK),
+        )
+        sq = sb.tile([P, Q], U32, name="sq", align_bytes=64)
+        sq_sc = sb.tile([P, Q], U8, name="sq_sc", align_bytes=64)
+        nc.vector.quantize_mx(
+            out=sq[:].bitcast(FP8X4), scales=sq_sc[:], in_=states_bf[:].rearrange("p q t -> p (q t)")
+        )
+        wq_dealt = sb.tile([P, K], U32, name="wq_dealt", align_bytes=64)
+        dealt_view = wq_dealt[:].rearrange("p (t m) -> p m t", t=PACK)
+        raw_view = wq_raw[:].rearrange("p (m t) -> p m t", t=PACK)
+        nc.scalar.copy(dealt_view[:, :, 0:2], raw_view[:, :, 0:2])
+        nc.vector.tensor_copy(wq_dealt[:].bitcast(I32).rearrange("p (t m) -> p m t", t=PACK)[:, :, 2:4],
+                              wq_raw[:].bitcast(I32).rearrange("p (m t) -> p m t", t=PACK)[:, :, 2:4])
+
+        qv_ps = psum.tile([P, PACK, Q], F32, name="qv_ps")
+        for t in range(PACK):
+            cols = slice(t * P, (t + 1) * P)
+            nc.tensor.matmul_mx(
+                out=qv_ps[:, t, :], lhsT=wq_dealt[:, cols].bitcast(FP8X4), lhsT_scale=wq_sc_dealt[:, cols],
+                rhs=sq[:].bitcast(FP8X4), rhs_scale=sq_sc[:], start=True, stop=True,
+            )
+        spread_scales(tags_sc, T)
+        spread_scales(cache_sc, T)
+        qv_bf = sb.tile([P, Q, PACK], BF16, name="qv_bf", align_bytes=64)
+        nc.scalar.copy(qv_bf[:], qv_ps[:].rearrange("p t q -> p q t"))
+        qq = sb.tile([P, Q], U32, name="qq", align_bytes=64)
+        qq_sc = sb.tile([P, Q], U8, name="qq_sc", align_bytes=64)
+        nc.vector.quantize_mx(
+            out=qq[:].bitcast(FP8X4), scales=qq_sc[:], in_=qv_bf[:].rearrange("p q t -> p (q t)")
+        )
+
+        banks = [psum.tile([P, NB], F32, name="a_ps%d" % b) for b in range(BANKS)]
+        for b in range(BANKS):
+            nc.tensor.matmul_mx(
+                out=banks[b][:], lhsT=sq[:].bitcast(FP8X4), lhsT_scale=sq_sc[:],
+                rhs=tags_w[:, 2 * b * NB : 2 * (b + 1) * NB].bitcast(FP4X4),
+                rhs_scale=tags_sc[:, b * NB : (b + 1) * NB], start=True, stop=False,
+            )
+        for b in range(BANKS):
+            nc.tensor.matmul_mx(
+                out=banks[b][:], lhsT=qq[:].bitcast(FP8X4), lhsT_scale=qq_sc[:],
+                rhs=cache_w[:, b * NB : (b + 1) * NB].bitcast(FP8X4),
+                rhs_scale=cache_sc[:, b * NB : (b + 1) * NB], start=False, stop=True,
+            )
+        for b in range(BANKS):
+            width = min(NB, T - 1 - b * NB)
+            dst = a1[:, b * NB + 1 : b * NB + 1 + width]
+            if b % 2 == 0:
+                nc.vector.tensor_copy(dst, banks[b][:, 0:width])
+            else:
+                nc.scalar.copy(dst, banks[b][:, 0:width])
+
+        g1a = sb.tile([P, HALF], F32, name="g1a", tag="slot_x")
+        nc.vector.tensor_copy(g1a[:], a1[:].indirect(entries(idx, 0, HALF)))
+        for b in range(BANKS // 2, BANKS):
+            nc.scalar.copy(a[:, b * NB : (b + 1) * NB], banks[b][:])
+        nc.scalar.activation(f2[:].indirect(entries(idx4, 0, HALF)), g1a[:], COPY)
+        nc.vector.tensor_copy(a[:, 0 : T // 2], a1[:, 1 : T // 2 + 1])
+        g2a = sb.tile([P, HALF], F32, name="g2a", tag="slot_y")
+        nc.vector.tensor_copy(g2a[:], a[:].indirect(entries(idx2, 0, HALF)))
+        wa = sb.tile([P, HALF], F32, name="wa")
+        nc.vector.tensor_max(wa[:], g1a[:], g2a[:])
+        nc.scalar.activation(f1[:].indirect(entries(idx3, 0, HALF)), wa[:], COPY)
+
+        g1b = sb.tile([P, HALF], F32, name="g1b", tag="slot_y")
+        nc.vector.tensor_copy(g1b[:], a1[:].indirect(entries(idx, HALF, I)))
+        g2b = sb.tile([P, HALF], F32, name="g2b", tag="slot_x")
+        nc.vector.tensor_copy(g2b[:], a[:].indirect(entries(idx2, HALF, I)))
+        wb = sb.tile([P, HALF], F32, name="wb")
+        nc.vector.tensor_max(wb[:], g1b[:], g2b[:])
+        nc.scalar.activation(f1[:].indirect(entries(idx3, HALF, I)), wb[:], COPY)
+
+        late = sb.tile([P, HALF + I], F32, name="late", tag="slot_x")
+        nc.vector.tensor_copy(late[:, 0:HALF], g1b[:])
+        nc.scalar.activation(f2[:].indirect(entries(idx4, HALF, I)), late[:, 0:HALF], COPY)
+        g4 = late[:, HALF : HALF + I]
+        nc.vector.tensor_copy(g4, a1[:].indirect(idx2[:]))
+
+        c1 = sb.tile([P, T], F32, name="c1")
+        nc.vector.tensor_sub(c1[:], a[:], f1[:])
+        c2 = sb.tile([P, T], F32, name="c2")
+        nc.vector.tensor_max(c2[:], c1[:], f2[:])
+
+        ya = sb.tile([P, HALF], F32, name="ya")
+        nc.vector.tensor_tensor(ya[:], c2[:].indirect(entries(idx5, 0, HALF)), g4[:, 0:HALF], ALU.add)
+        nc.sync.dma_start(out[:, 0:HALF], ya[:])
+        g5b = sb.tile([P, HALF], F32, name="g5b")
+        nc.scalar.activation(g5b[:], c2[:].indirect(entries(idx5, HALF, I)), COPY)
+        yb = sb.tile([P, HALF], F32, name="yb")
+        nc.vector.tensor_add(yb[:], g5b[:], g4[:, HALF:I])
+        nc.sync.dma_start(out[:, HALF:I], yb[:])

@@ -22,6 +22,7 @@ BANKS = 4
 NB = T // BANKS
 HALF = I // 2
 LANES = 16
+MID = 64
 
 
 def entries(list_tile, lo, hi):
@@ -39,43 +40,37 @@ def tile_attend_nexttoken_parts_kernel(
         psum = ctx.enter_context(tc.psum_pool(name="psum", bufs=1))
 
         def scale_tile(name, width):
-            plane = sb.tile([P, 2 * width], U8, name=name, align_bytes=64)
+            plane = sb.tile([P, width], U8, name=name, tag=name, align_bytes=64)
             nc.vector.memset(plane[:].bitcast(I32), 0)
             return plane
 
-        def load_scales(queue, plane, scales):
+        def load_scale_pairs(queue, plane, scales, base):
             rows = scales[0].bitcast(I32).rearrange("(h g r) n -> g r h n", h=2, g=2)
             for g in range(2):
-                queue.dma_start(
-                    plane[32 * g : 32 * g + 4, :].bitcast(I32).rearrange("r (h n) -> r h n", h=2), rows[g]
-                )
+                first = base + 32 * g
+                queue.dma_start(plane[first : first + 4, :].bitcast(I32).rearrange("r (h n) -> r h n", h=2), rows[g])
 
-        def spread_scales(plane, width):
-            words = plane[:].bitcast(I32)
-            n = width // 4
-            nc.vector.tensor_copy(words[64:128, 0:n], words[0:64, n : 2 * n])
-
-        wq_sc = scale_tile("wq_sc", K)
-        tags_sc = scale_tile("tags_sc", T)
-        cache_sc = scale_tile("cache_sc", T)
+        wq_sc = scale_tile("wq_sc", 2 * K)
+        tags_sc = scale_tile("tags_sc", 2 * T)
+        cache_sc = scale_tile("cache_sc", NB)
         zero = sb.tile([P, 1], F32, name="zero")
         nc.vector.memset(zero[:], 0.0)
         f1 = sb.tile([P, T], F32, name="f1")
-        f2 = sb.tile([P, T], F32, name="f2")
-        nc.vector.memset(f2[:], 0.0)
         nc.vector.memset(f1[:], 0.0)
 
-        states_raw = sb.tile([P, PACK, Q], F32, name="states_raw")
+        states_raw = sb.tile([P, PACK, Q], F32, name="states_raw", tag="slot_s", align_bytes=64)
         nc.sync.dma_start(states_raw[:], states.rearrange("(p t) q -> p t q", t=PACK))
-        load_scales(nc.scalar, wq_sc, wq_scales)
+        load_scale_pairs(nc.scalar, wq_sc, wq_scales, 64)
         wq_raw = sb.tile([P, K], U32, name="wq_raw")
         nc.sync.dma_start(wq_raw[:].bitcast(I32), wq_words[0].rearrange("p n t -> p (n t)").bitcast(I32))
-        load_scales(nc.scalar, tags_sc, tags_scales)
+        load_scale_pairs(nc.sync, tags_sc, tags_scales, 0)
         tags_w = sb.tile([P, 2 * T], U8, name="tags_w", align_bytes=64)
         nc.sync.dma_start(tags_w[:].bitcast(I32), tags_words[0].bitcast(I32))
-        load_scales(nc.sync, cache_sc, cache_scales)
         cache_w = sb.tile([P, T], U32, name="cache_w", align_bytes=64)
         nc.sync.dma_start(cache_w[:].bitcast(I32), cache_words[0].rearrange("p n t -> p (n t)").bitcast(I32))
+        cache_rows = cache_scales[0].bitcast(I32).rearrange("(g r) (b n) -> g b r n", r=4, b=BANKS)
+        for g in range(4):
+            nc.sync.dma_start(cache_sc[32 * g : 32 * g + 4 * BANKS, :].bitcast(I32), cache_rows[g])
         held = []
         for name, src in (("idx", offs), ("idx4", offs4), ("idx2", offs2), ("idx3", offs3), ("idx5", offs5)):
             list_tile = lists.tile([P, I // LANES], U16, name=name)
@@ -87,26 +82,35 @@ def tile_attend_nexttoken_parts_kernel(
         a1 = sb.tile([P, T], F32, name="a1")
         nc.scalar.activation(a1[:, 0:1], zero[:], COPY)
 
-        spread_scales(wq_sc, K)
         states_bf = sb.tile([P, Q, PACK], BF16, name="states_bf", align_bytes=64)
-        nc.vector.tensor_copy(states_bf[:], states_raw[:].rearrange("p t q -> p q t"))
-        wq_sc_dealt = sb.tile([P, K], U8, name="wq_sc_dealt", align_bytes=64)
-        nc.vector.tensor_copy(
-            wq_sc_dealt[:].rearrange("p (t m) -> p m t", t=PACK),
-            wq_sc[:, 0:K].rearrange("p (m t) -> p m t", t=PACK),
-        )
         sq = sb.tile([P, Q], U32, name="sq", align_bytes=64)
         sq_sc = sb.tile([P, Q], U8, name="sq_sc", align_bytes=64)
-        nc.vector.quantize_mx(
-            out=sq[:].bitcast(FP8X4), scales=sq_sc[:], in_=states_bf[:].rearrange("p q t -> p (q t)")
-        )
+        halves = [slice(0, Q // 2), slice(Q // 2, Q)]
+        nc.vector.tensor_copy(states_bf[:, halves[0], :], states_raw[:, :, halves[0]].rearrange("p t q -> p q t"))
+        nc.scalar.copy(states_bf[:, halves[1], :], states_raw[:, :, halves[1]].rearrange("p t q -> p q t"))
+        wq_sc_words = wq_sc[:].bitcast(I32)
+        nc.vector.tensor_copy(wq_sc_words[0:64, K // 4 : K // 2], wq_sc_words[64:128, 0 : K // 4])
+        for rows in halves:
+            nc.vector.quantize_mx(
+                out=sq[:, rows].bitcast(FP8X4), scales=sq_sc[:, rows],
+                in_=states_bf[:, rows, :].rearrange("p q t -> p (q t)"),
+            )
+        wq_sc_dealt = sb.tile([P, K], U8, name="wq_sc_dealt", tag="slot_s", align_bytes=64)
         wq_dealt = sb.tile([P, K], U32, name="wq_dealt", align_bytes=64)
-        dealt_view = wq_dealt[:].rearrange("p (t m) -> p m t", t=PACK)
-        raw_view = wq_raw[:].rearrange("p (m t) -> p m t", t=PACK)
-        nc.scalar.copy(dealt_view[:, :, 0:2], raw_view[:, :, 0:2])
-        nc.vector.tensor_copy(wq_dealt[:].bitcast(I32).rearrange("p (t m) -> p m t", t=PACK)[:, :, 2:4],
-                              wq_raw[:].bitcast(I32).rearrange("p (m t) -> p m t", t=PACK)[:, :, 2:4])
+        for t in range(0, PACK, 2):
+            nc.vector.tensor_copy(
+                wq_sc_dealt[:].rearrange("p (t m) -> p m t", t=PACK)[:, :, t : t + 2],
+                wq_sc[:, K : 2 * K].rearrange("p (m t) -> p m t", t=PACK)[:, :, t : t + 2],
+            )
+            nc.scalar.copy(
+                wq_dealt[:].rearrange("p (t m) -> p m t", t=PACK)[:, :, t : t + 2],
+                wq_raw[:].rearrange("p (m t) -> p m t", t=PACK)[:, :, t : t + 2],
+            )
+        tags_sc_words = tags_sc[:].bitcast(I32)
+        nc.vector.tensor_copy(tags_sc_words[64:128, 0 : T // 4], tags_sc_words[0:64, T // 4 : T // 2])
 
+        f2 = sb.tile([P, T], F32, name="f2", tag="wq_sc", align_bytes=64)
+        nc.vector.memset(f2[:], 0.0)
         qv_ps = psum.tile([P, PACK, Q], F32, name="qv_ps")
         for t in range(PACK):
             cols = slice(t * P, (t + 1) * P)
@@ -114,8 +118,6 @@ def tile_attend_nexttoken_parts_kernel(
                 out=qv_ps[:, t, :], lhsT=wq_dealt[:, cols].bitcast(FP8X4), lhsT_scale=wq_sc_dealt[:, cols],
                 rhs=sq[:].bitcast(FP8X4), rhs_scale=sq_sc[:], start=True, stop=True,
             )
-        spread_scales(tags_sc, T)
-        spread_scales(cache_sc, T)
         qv_bf = sb.tile([P, Q, PACK], BF16, name="qv_bf", align_bytes=64)
         nc.scalar.copy(qv_bf[:], qv_ps[:].rearrange("p t q -> p q t"))
         qq = sb.tile([P, Q], U32, name="qq", align_bytes=64)
@@ -124,33 +126,33 @@ def tile_attend_nexttoken_parts_kernel(
             out=qq[:].bitcast(FP8X4), scales=qq_sc[:], in_=qv_bf[:].rearrange("p q t -> p (q t)")
         )
 
-        banks = [psum.tile([P, NB], F32, name="a_ps%d" % b) for b in range(BANKS)]
-        for b in range(BANKS):
+        spans = [(0, 256), (256, 512), (512, 768), (768, 896), (896, 1024)]
+        banks = [psum.tile([P, hi - lo], F32, name="a_ps%d" % lo) for lo, hi in spans]
+        for bank, (lo, hi) in zip(banks, spans):
             nc.tensor.matmul_mx(
-                out=banks[b][:], lhsT=sq[:].bitcast(FP8X4), lhsT_scale=sq_sc[:],
-                rhs=tags_w[:, 2 * b * NB : 2 * (b + 1) * NB].bitcast(FP4X4),
-                rhs_scale=tags_sc[:, b * NB : (b + 1) * NB], start=True, stop=False,
+                out=bank[:], lhsT=sq[:].bitcast(FP8X4), lhsT_scale=sq_sc[:],
+                rhs=tags_w[:, 2 * lo : 2 * hi].bitcast(FP4X4), rhs_scale=tags_sc[:, lo:hi], start=True, stop=False,
             )
-        for b in range(BANKS):
+        for bank, (lo, hi) in zip(banks, spans):
+            block = lo // NB
             nc.tensor.matmul_mx(
-                out=banks[b][:], lhsT=qq[:].bitcast(FP8X4), lhsT_scale=qq_sc[:],
-                rhs=cache_w[:, b * NB : (b + 1) * NB].bitcast(FP8X4),
-                rhs_scale=cache_sc[:, b * NB : (b + 1) * NB], start=False, stop=True,
+                out=bank[:], lhsT=qq[:].bitcast(FP8X4), lhsT_scale=qq_sc[:],
+                rhs=cache_w[:, lo:hi].bitcast(FP8X4),
+                rhs_scale=cache_sc[4 * block : P, lo - block * NB : hi - block * NB], start=False, stop=True,
             )
-        for b in range(BANKS):
-            width = min(NB, T - 1 - b * NB)
-            dst = a1[:, b * NB + 1 : b * NB + 1 + width]
-            if b % 2 == 0:
+        for b, (lo, hi) in enumerate(spans):
+            width = min(hi, T - 1) - lo
+            dst = a1[:, lo + 1 : lo + 1 + width]
+            if b in (0, 2):
                 nc.vector.tensor_copy(dst, banks[b][:, 0:width])
             else:
                 nc.scalar.copy(dst, banks[b][:, 0:width])
-
+        nc.vector.tensor_copy(a[:, 0 : T // 2], a1[:, 1 : T // 2 + 1])
         g1a = sb.tile([P, HALF], F32, name="g1a", tag="slot_x")
         nc.vector.tensor_copy(g1a[:], a1[:].indirect(entries(idx, 0, HALF)))
-        for b in range(BANKS // 2, BANKS):
-            nc.scalar.copy(a[:, b * NB : (b + 1) * NB], banks[b][:])
+        for bank, (lo, hi) in list(zip(banks, spans))[2:]:
+            nc.scalar.copy(a[:, lo:hi], bank[:])
         nc.scalar.activation(f2[:].indirect(entries(idx4, 0, HALF)), g1a[:], COPY)
-        nc.vector.tensor_copy(a[:, 0 : T // 2], a1[:, 1 : T // 2 + 1])
         g2a = sb.tile([P, HALF], F32, name="g2a", tag="slot_y")
         nc.vector.tensor_copy(g2a[:], a[:].indirect(entries(idx2, 0, HALF)))
         wa = sb.tile([P, HALF], F32, name="wa")
@@ -159,6 +161,7 @@ def tile_attend_nexttoken_parts_kernel(
 
         g1b = sb.tile([P, HALF], F32, name="g1b", tag="slot_y")
         nc.vector.tensor_copy(g1b[:], a1[:].indirect(entries(idx, HALF, I)))
+        nc.scalar.activation(f2[:].indirect(entries(idx4, HALF, HALF + MID)), g1b[:, 0:MID], COPY)
         g2b = sb.tile([P, HALF], F32, name="g2b", tag="slot_x")
         nc.vector.tensor_copy(g2b[:], a[:].indirect(entries(idx2, HALF, I)))
         wb = sb.tile([P, HALF], F32, name="wb")
@@ -166,15 +169,17 @@ def tile_attend_nexttoken_parts_kernel(
         nc.scalar.activation(f1[:].indirect(entries(idx3, HALF, I)), wb[:], COPY)
 
         late = sb.tile([P, HALF + I], F32, name="late", tag="slot_x")
-        nc.vector.tensor_copy(late[:, 0:HALF], g1b[:])
-        nc.scalar.activation(f2[:].indirect(entries(idx4, HALF, I)), late[:, 0:HALF], COPY)
+        nc.vector.tensor_copy(late[:, MID:HALF], g1b[:, MID:HALF])
+        nc.scalar.activation(f2[:].indirect(entries(idx4, HALF + MID, I)), late[:, MID:HALF], COPY)
         g4 = late[:, HALF : HALF + I]
         nc.vector.tensor_copy(g4, a1[:].indirect(idx2[:]))
 
         c1 = sb.tile([P, T], F32, name="c1")
-        nc.vector.tensor_sub(c1[:], a[:], f1[:])
+        for cols in (slice(0, T // 2), slice(T // 2, T)):
+            nc.vector.tensor_sub(c1[:, cols], a[:, cols], f1[:, cols])
         c2 = sb.tile([P, T], F32, name="c2")
-        nc.vector.tensor_max(c2[:], c1[:], f2[:])
+        for cols in (slice(0, T // 2), slice(T // 2, T)):
+            nc.vector.tensor_max(c2[:, cols], c1[:, cols], f2[:, cols])
 
         ya = sb.tile([P, HALF], F32, name="ya")
         nc.vector.tensor_tensor(ya[:], c2[:].indirect(entries(idx5, 0, HALF)), g4[:, 0:HALF], ALU.add)

@@ -66,11 +66,13 @@ def tile_attend_nexttoken_parts_kernel(
         load_scale_pairs(nc.sync, tags_sc, tags_scales, 0)
         tags_w = sb.tile([P, 2 * T], U8, name="tags_w", align_bytes=64)
         nc.sync.dma_start(tags_w[:].bitcast(I32), tags_words[0].bitcast(I32))
-        cache_w = sb.tile([P, T], U32, name="cache_w", align_bytes=64)
-        nc.sync.dma_start(cache_w[:].bitcast(I32), cache_words[0].rearrange("p n t -> p (n t)").bitcast(I32))
+        cache_src = cache_words[0].rearrange("p n t -> p (n t)").bitcast(I32)
+        cache_w = [sb.tile([P, T // 2], U32, name="cache_w%d" % h, align_bytes=64) for h in range(2)]
+        nc.sync.dma_start(cache_w[0][:].bitcast(I32), cache_src[:, 0 : T // 2])
         cache_rows = cache_scales[0].bitcast(I32).rearrange("(g r) (b n) -> g b r n", r=4, b=BANKS)
         for g in range(4):
             nc.sync.dma_start(cache_sc[32 * g : 32 * g + 4 * BANKS, :].bitcast(I32), cache_rows[g])
+        nc.sync.dma_start(cache_w[1][:].bitcast(I32), cache_src[:, T // 2 : T])
         held = []
         for name, src in (("idx", offs), ("idx4", offs4), ("idx2", offs2), ("idx3", offs3), ("idx5", offs5)):
             list_tile = lists.tile([P, I // LANES], U16, name=name)
@@ -137,7 +139,7 @@ def tile_attend_nexttoken_parts_kernel(
             block = lo // NB
             nc.tensor.matmul_mx(
                 out=bank[:], lhsT=qq[:].bitcast(FP8X4), lhsT_scale=qq_sc[:],
-                rhs=cache_w[:, lo:hi].bitcast(FP8X4),
+                rhs=cache_w[lo // (T // 2)][:, lo % (T // 2) : lo % (T // 2) + hi - lo].bitcast(FP8X4),
                 rhs_scale=cache_sc[4 * block : P, lo - block * NB : hi - block * NB], start=False, stop=True,
             )
         for b, (lo, hi) in enumerate(spans):

from contextlib import ExitStack

import concourse.mybir as mybir

D, K, T, I, Q = 512, 512, 1024, 512, 128
FLOPS = 2 * (D * K * Q + K * Q * T + D * Q * T)

F32 = mybir.dt.float32
BF16 = mybir.dt.bfloat16
I32 = mybir.dt.int32
U32 = mybir.dt.uint32
U16 = mybir.dt.uint16
U8 = mybir.dt.uint8
FP8X4 = mybir.dt.float8_e4m3fn_x4
FP4X4 = mybir.dt.float4_e2m1fn_x4
COPY = mybir.ActivationFunctionType.Copy
ALU = mybir.AluOpType

P = 128
PACK = 4
BANKS = 4
NB = T // BANKS
HALF = I // 2
LANES = 16
MID = 64


def entries(list_tile, lo, hi):
    return list_tile[:, lo // LANES : hi // LANES]


def tile_attend_nexttoken_parts_kernel(
    tc, states, wq_words, wq_scales, cache_words, cache_scales, tags_words, tags_scales,
    offs, offs2, offs3, offs4, offs5, out,
):
    nc = tc.nc
    with ExitStack() as ctx:
        lists = ctx.enter_context(tc.tile_pool(name="lists", bufs=1))
        sb = ctx.enter_context(tc.tile_pool(name="sb", bufs=1))
        psum = ctx.enter_context(tc.psum_pool(name="psum", bufs=1))

        def scale_tile(name, width):
            plane = sb.tile([P, width], U8, name=name, tag=name, align_bytes=64)
            nc.vector.memset(plane[:].bitcast(I32), 0)
            return plane

        def load_scale_pairs(queue, plane, scales, base):
            rows = scales[0].bitcast(I32).rearrange("(h g r) n -> g r h n", h=2, g=2)
            for g in range(2):
                first = base + 32 * g
                queue.dma_start(plane[first : first + 4, :].bitcast(I32).rearrange("r (h n) -> r h n", h=2), rows[g])

        wq_sc = scale_tile("wq_sc", 2 * K)
        tags_sc = scale_tile("tags_sc", 2 * T)
        cache_sc = scale_tile("cache_sc", NB)
        zero = sb.tile([P, 1], F32, name="zero")
        nc.vector.memset(zero[:], 0.0)
        f1 = sb.tile([P, T], F32, name="f1")
        nc.vector.memset(f1[:], 0.0)

        states_raw = sb.tile([P, PACK, Q], F32, name="states_raw", tag="slot_s", align_bytes=64)
        nc.sync.dma_start(states_raw[:], states.rearrange("(p t) q -> p t q", t=PACK))
        load_scale_pairs(nc.scalar, wq_sc, wq_scales, 64)
        wq_raw = sb.tile([P, K], U32, name="wq_raw")
        nc.sync.dma_start(wq_raw[:].bitcast(I32), wq_words[0].rearrange("p n t -> p (n t)").bitcast(I32))
        load_scale_pairs(nc.sync, tags_sc, tags_scales, 0)
        tags_w = sb.tile([P, 2 * T], U8, name="tags_w", align_bytes=64)
        nc.sync.dma_start(tags_w[:].bitcast(I32), tags_words[0].bitcast(I32))
        cache_src = cache_words[0].rearrange("p n t -> p (n t)").bitcast(I32)
        cache_w = [sb.tile([P, T // 2], U32, name="cache_w%d" % h, align_bytes=64) for h in range(2)]
        nc.sync.dma_start(cache_w[0][:].bitcast(I32), cache_src[:, 0 : T // 2])
        cache_rows = cache_scales[0].bitcast(I32).rearrange("(g r) (b n) -> g b r n", r=4, b=BANKS)
        for g in range(4):
            nc.sync.dma_start(cache_sc[32 * g : 32 * g + 4 * BANKS, :].bitcast(I32), cache_rows[g])
        nc.sync.dma_start(cache_w[1][:].bitcast(I32), cache_src[:, T // 2 : T])
        held = []
        for name, src in (("idx", offs), ("idx4", offs4), ("idx2", offs2), ("idx3", offs3), ("idx5", offs5)):
            list_tile = lists.tile([P, I // LANES], U16, name=name)
            nc.sync.dma_start(list_tile[:], src)
            held.append(list_tile)
        idx, idx4, idx2, idx3, idx5 = held

        a = sb.tile([P, T], F32, name="a")
        a1 = sb.tile([P, T], F32, name="a1")
        nc.scalar.activation(a1[:, 0:1], zero[:], COPY)

        states_bf = sb.tile([P, Q, PACK], BF16, name="states_bf", align_bytes=64)
        sq = sb.tile([P, Q], U32, name="sq", align_bytes=64)
        sq_sc = sb.tile([P, Q], U8, name="sq_sc", align_bytes=64)
        halves = [slice(0, Q // 2), slice(Q // 2, Q)]
        nc.vector.tensor_copy(states_bf[:, halves[0], :], states_raw[:, :, halves[0]].rearrange("p t q -> p q t"))
        nc.scalar.copy(states_bf[:, halves[1], :], states_raw[:, :, halves[1]].rearrange("p t q -> p q t"))
        wq_sc_words = wq_sc[:].bitcast(I32)
        nc.vector.tensor_copy(wq_sc_words[0:64, K // 4 : K // 2], wq_sc_words[64:128, 0 : K // 4])
        for rows in halves:
            nc.vector.quantize_mx(
                out=sq[:, rows].bitcast(FP8X4), scales=sq_sc[:, rows],
                in_=states_bf[:, rows, :].rearrange("p q t -> p (q t)"),
            )
        wq_sc_dealt = sb.tile([P, K], U8, name="wq_sc_dealt", tag="slot_s", align_bytes=64)
        wq_dealt = sb.tile([P, K], U32, name="wq_dealt", align_bytes=64)
        for t in range(0, PACK, 2):
            nc.vector.tensor_copy(
                wq_sc_dealt[:].rearrange("p (t m) -> p m t", t=PACK)[:, :, t : t + 2],
                wq_sc[:, K : 2 * K].rearrange("p (m t) -> p m t", t=PACK)[:, :, t : t + 2],
            )
            nc.scalar.copy(
                wq_dealt[:].rearrange("p (t m) -> p m t", t=PACK)[:, :, t : t + 2],
                wq_raw[:].rearrange("p (m t) -> p m t", t=PACK)[:, :, t : t + 2],
            )
        tags_sc_words = tags_sc[:].bitcast(I32)
        nc.vector.tensor_copy(tags_sc_words[64:128, 0 : T // 4], tags_sc_words[0:64, T // 4 : T // 2])

        f2 = sb.tile([P, T], F32, name="f2", tag="wq_sc", align_bytes=64)
        nc.vector.memset(f2[:], 0.0)
        qv_ps = psum.tile([P, PACK, Q], F32, name="qv_ps")
        for t in range(PACK):
            cols = slice(t * P, (t + 1) * P)
            nc.tensor.matmul_mx(
                out=qv_ps[:, t, :], lhsT=wq_dealt[:, cols].bitcast(FP8X4), lhsT_scale=wq_sc_dealt[:, cols],
                rhs=sq[:].bitcast(FP8X4), rhs_scale=sq_sc[:], start=True, stop=True,
            )
        qv_bf = sb.tile([P, Q, PACK], BF16, name="qv_bf", align_bytes=64)
        nc.scalar.copy(qv_bf[:], qv_ps[:].rearrange("p t q -> p q t"))
        qq = sb.tile([P, Q], U32, name="qq", align_bytes=64)
        qq_sc = sb.tile([P, Q], U8, name="qq_sc", align_bytes=64)
        nc.vector.quantize_mx(
            out=qq[:].bitcast(FP8X4), scales=qq_sc[:], in_=qv_bf[:].rearrange("p q t -> p (q t)")
        )

        spans = [(0, 256), (256, 512), (512, 768), (768, 896), (896, 1024)]
        banks = [psum.tile([P, hi - lo], F32, name="a_ps%d" % lo) for lo, hi in spans]
        for bank, (lo, hi) in zip(banks, spans):
            nc.tensor.matmul_mx(
                out=bank[:], lhsT=sq[:].bitcast(FP8X4), lhsT_scale=sq_sc[:],
                rhs=tags_w[:, 2 * lo : 2 * hi].bitcast(FP4X4), rhs_scale=tags_sc[:, lo:hi], start=True, stop=False,
            )
        for bank, (lo, hi) in zip(banks, spans):
            block = lo // NB
            nc.tensor.matmul_mx(
                out=bank[:], lhsT=qq[:].bitcast(FP8X4), lhsT_scale=qq_sc[:],
                rhs=cache_w[lo // (T // 2)][:, lo % (T // 2) : lo % (T // 2) + hi - lo].bitcast(FP8X4),
                rhs_scale=cache_sc[4 * block : P, lo - block * NB : hi - block * NB], start=False, stop=True,
            )
        for b, (lo, hi) in enumerate(spans):
            width = min(hi, T - 1) - lo
            dst = a1[:, lo + 1 : lo + 1 + width]
            if b in (0, 2):
                nc.vector.tensor_copy(dst, banks[b][:, 0:width])
            else:
                nc.scalar.copy(dst, banks[b][:, 0:width])
        nc.vector.tensor_copy(a[:, 0 : T // 2], a1[:, 1 : T // 2 + 1])
        g1a = sb.tile([P, HALF], F32, name="g1a", tag="slot_x")
        nc.vector.tensor_copy(g1a[:], a1[:].indirect(entries(idx, 0, HALF)))
        for bank, (lo, hi) in list(zip(banks, spans))[2:]:
            nc.scalar.copy(a[:, lo:hi], bank[:])
        nc.scalar.activation(f2[:].indirect(entries(idx4, 0, HALF)), g1a[:], COPY)
        g2a = sb.tile([P, HALF], F32, name="g2a", tag="slot_y")
        nc.vector.tensor_copy(g2a[:], a[:].indirect(entries(idx2, 0, HALF)))
        wa = sb.tile([P, HALF], F32, name="wa")
        nc.vector.tensor_max(wa[:], g1a[:], g2a[:])
        nc.scalar.activation(f1[:].indirect(entries(idx3, 0, HALF)), wa[:], COPY)

        g1b = sb.tile([P, HALF], F32, name="g1b", tag="slot_y")
        nc.vector.tensor_copy(g1b[:], a1[:].indirect(entries(idx, HALF, I)))
        nc.scalar.activation(f2[:].indirect(entries(idx4, HALF, HALF + MID)), g1b[:, 0:MID], COPY)
        g2b = sb.tile([P, HALF], F32, name="g2b", tag="slot_x")
        nc.vector.tensor_copy(g2b[:], a[:].indirect(entries(idx2, HALF, I)))
        wb = sb.tile([P, HALF], F32, name="wb")
        nc.vector.tensor_max(wb[:], g1b[:], g2b[:])
        nc.scalar.activation(f1[:].indirect(entries(idx3, HALF, I)), wb[:], COPY)

        late = sb.tile([P, HALF + I], F32, name="late", tag="slot_x")
        nc.vector.tensor_copy(late[:, MID:HALF], g1b[:, MID:HALF])
        nc.scalar.activation(f2[:].indirect(entries(idx4, HALF + MID, I)), late[:, MID:HALF], COPY)
        g4 = late[:, HALF : HALF + I]
        nc.vector.tensor_copy(g4, a1[:].indirect(idx2[:]))

        c1 = sb.tile([P, T], F32, name="c1")
        for cols in (slice(0, T // 2), slice(T // 2, T)):
            nc.vector.tensor_sub(c1[:, cols], a[:, cols], f1[:, cols])
        c2 = sb.tile([P, T], F32, name="c2")
        for cols in (slice(0, T // 2), slice(T // 2, T)):
            nc.vector.tensor_max(c2[:, cols], c1[:, cols], f2[:, cols])

        ya = sb.tile([P, HALF], F32, name="ya")
        nc.vector.tensor_tensor(ya[:], c2[:].indirect(entries(idx5, 0, HALF)), g4[:, 0:HALF], ALU.add)
        nc.sync.dma_start(out[:, 0:HALF], ya[:])
        g5b = sb.tile([P, HALF], F32, name="g5b")
        nc.scalar.activation(g5b[:], c2[:].indirect(entries(idx5, HALF, I)), COPY)
        yb = sb.tile([P, HALF], F32, name="yb")
        nc.vector.tensor_add(yb[:], g5b[:], g4[:, HALF:I])
        nc.sync.dma_start(out[:, HALF:I], yb[:])
